import numpy as np
import ml_dtypes


def mxq(x, axis, fmt="e4m3"):
    dtype, down = {"e4m3": (ml_dtypes.float8_e4m3fn, 7), "e5m2": (ml_dtypes.float8_e5m2, 14)}[fmt]
    v = np.moveaxis(np.asarray(x, np.float32).astype(ml_dtypes.bfloat16).astype(np.float64), axis, -1)
    blocks = v.reshape(v.shape[:-1] + (-1, 32))
    amax = np.abs(blocks).max(-1, keepdims=True)
    byte = np.maximum(np.where(amax > 0, np.frexp(amax)[1] - 1 + 127, 0) - down, 1)
    scale = np.exp2(byte - 127.0)
    codes = (blocks / scale).astype(np.float32).astype(dtype).astype(np.float64)
    return np.moveaxis((codes * scale).reshape(v.shape), -1, axis)


WIDE = False


def mx_kscale(k):
    if not WIDE:
        return np.ones(k)
    levels = np.array([10, -10, 5, -5, 0])
    if k % 512:
        return np.exp2(np.random.permutation(np.resize(levels, k // 32))).repeat(32)
    a = np.empty((k // 512, 16))
    for p in range(k // 512):
        a[p, :8] = np.random.permutation(np.resize(levels, 8))
        for g in range(8):
            far = levels[np.abs(levels - a[p, g]) >= 10]
            a[p, g + 8] = far[np.random.randint(len(far))]
    return np.exp2(a.ravel()).repeat(32)


def f64(x):
    return np.asarray(x).astype(np.float64)


def striped(idx):
    return np.tile(np.asarray(idx).reshape(-1, 16).T, (8, 1)).astype(np.uint16)


def unstriped(offs):
    return offs[:16].T.reshape(-1).astype(np.int64)


E2M1 = np.array([0.0, 0.5, 1.0, 1.5, 2.0, 3.0, 4.0, 6.0, -0.0, -0.5, -1.0, -1.5, -2.0, -3.0, -4.0, -6.0])


def pack_weight(w, fmt):
    k, n = w.shape
    w = f64(np.asarray(w, np.float32).astype(ml_dtypes.bfloat16)).reshape(k // 32, 32, n)
    amax = np.abs(w).max(1)
    if fmt == "e4m3":
        byte = np.frexp(amax)[1] - 1 + 127 - 7
    else:
        mant, ex = np.frexp(amax / 6.0)
        byte = np.where(mant > 0.5, ex, ex - 1) + 127
    byte = np.clip(np.where(amax > 0, byte, 1), 1, 254)
    scaled = (w * np.exp2(127.0 - byte)[:, None, :]).reshape(k, n).astype(np.float32)
    by_word = np.ascontiguousarray(scaled.reshape(k // 512, 128, 4, n).transpose(0, 1, 3, 2))
    if fmt == "e4m3":
        words = by_word.astype(ml_dtypes.float8_e4m3fn).view(np.uint8)
    else:
        c = by_word.astype(ml_dtypes.float4_e2m1fn).view(np.uint8) & 0xF
        words = (c[..., 0::2] | (c[..., 1::2] << 4)).reshape(k // 512, 128, 2 * n)
    return np.ascontiguousarray(words), np.ascontiguousarray(byte.astype(np.uint8).reshape(k // 512, 16, n))


def unpack_weight(words, scales, fmt):
    g, _, n = scales.shape
    words = np.ascontiguousarray(words).reshape(g, 128, n, -1)
    if fmt == "e4m3":
        vals = words.view(ml_dtypes.float8_e4m3fn).astype(np.float64)
    else:
        nib = np.empty((g, 128, n, 4), np.uint8)
        nib[..., 0::2] = words & 0xF
        nib[..., 1::2] = words >> 4
        vals = E2M1[nib]
    vals = vals * np.repeat(np.exp2(scales.astype(np.float64) - 127.0), 8, axis=1)[..., None]
    return vals.transpose(0, 1, 3, 2).reshape(g * 512, n)


def bf(x):
    return np.asarray(x, np.float32).astype(ml_dtypes.bfloat16)


def planes(Y):
    r, m = Y.shape
    b = f64(bf(Y)).reshape(r // 32, 32, m)
    amax = np.abs(b).max(1)
    byte = np.clip(np.where(amax > 0, np.frexp(amax)[1] - 1 + 127 - 7, 1), 1, 254)
    codes = (b * np.exp2(127.0 - byte)[:, None, :]).reshape(r, m).astype(np.float32).astype(ml_dtypes.float8_e4m3fn).view(np.uint8)
    words = codes.reshape(r // 512, 128, 4, m).transpose(0, 1, 3, 2)
    return np.ascontiguousarray(words), np.ascontiguousarray(byte.astype(np.uint8).reshape(r // 512, 16, m))


D, E, T, I, U, Q = 512, 512, 2048, 256, 1024, 512


def setup_inputs():
    n = np.random.standard_normal
    idx = np.random.permutation(T)[:I]
    idx2 = np.random.permutation(U)[:I]
    fd = mx_kscale(D)
    fe = mx_kscale(E)
    fq = mx_kscale(Q)
    keysp = pack_weight(n((D, T)) / fd[:, None], "e4m3")
    valsp = pack_weight(n((E, T)) / fe[:, None], "e4m3")
    return {
        "query": (n((D, Q)) * 0.5 / np.sqrt(D) * fd[:, None]).astype(np.float32),
        "keys_words": keysp[0],
        "keys_scales": keysp[1],
        "gout": (n((E, Q)) * 1 / np.sqrt(E) * fe[:, None]).astype(np.float32),
        "vals_words": valsp[0],
        "vals_scales": valsp[1],
        "lse": (np.random.uniform(6.2, 6.5, (Q, 1))).astype(np.float32),
        "delta": (np.random.uniform(-0.3, 0.3, (Q, 1))).astype(np.float32),
        "qs": (np.random.uniform(100.0, 400.0, (Q, 1)) * fq[:, None]).astype(np.float32),
        "qrows": (n((Q, D)) / fq[:, None]).astype(np.float32),
        "old": (n((D, U)) * 4.0).astype(np.float32),
        "fade": (np.random.uniform(0.5, 1.0, (1, U))).astype(np.float32),
        "offs": striped(idx),
        "offs2": striped(idx2),
    }


def reference(query, keys_words, keys_scales, gout, vals_words, vals_scales, lse, delta, qs, qrows, old, fade, offs, offs2):
    idx = unstriped(offs)
    idx2 = unstriped(offs2)
    keysu = unpack_weight(keys_words, keys_scales, "e4m3")
    valsu = unpack_weight(vals_words, vals_scales, "e4m3")
    queryq = mxq(f64(query), 0, "e4m3")
    keysidxg = keysu[:, idx]
    a = queryq.T @ keysidxg
    goutq = mxq(f64(gout), 0, "e4m3")
    valsidxg = valsu[:, idx]
    dp = goutq.T @ valsidxg
    ds = np.exp(a - f64(lse)) * (dp - f64(delta)) * f64(qs)
    qrowsq = mxq(f64(qrows), 0, "e4m3")
    dsq = mxq(ds, 0, "e4m3")
    dk = qrowsq.T @ dsq
    df = np.zeros((D, U))
    df[:, idx2] = dk
    y = f64(old) * f64(fade) + df
    words, scales = planes(y)
    return y, words, scales

@@ -1,0 +1,212 @@
+from contextlib import ExitStack
+
+import concourse.mybir as mybir
+from concourse.masks import make_identity
+
+F32 = mybir.dt.float32
+BF16 = mybir.dt.bfloat16
+I32 = mybir.dt.int32
+U32 = mybir.dt.uint32
+U16 = mybir.dt.uint16
+U8 = mybir.dt.uint8
+FP8X4 = mybir.dt.float8_e4m3fn_x4
+ALU = mybir.AluOpType
+ACT = mybir.ActivationFunctionType
+
+P = 128
+PACK = 4
+D, E, T, SLOTS, U, Q = 512, 512, 2048, 256, 1024, 512
+HALF = U // 2
+QUARTER = U // 4
+BANK = 512
+VAL_ROW = 4
+
+FLOPS = 2 * Q * SLOTS * (D + E + D)
+
+
+def tile_attend_gkeystore_pl_kernel(tc, query, keys_words, keys_scales, gout, vals_words, vals_scales, lse, delta, qs,
+                                     qrows, old, fade, offs, offs2, out_0, out_1, out_2):
+    nc = tc.nc
+    with ExitStack() as ctx:
+        sb = ctx.enter_context(tc.tile_pool(name="sb", bufs=1))
+        ps = ctx.enter_context(tc.psum_pool(name="ps", bufs=1))
+
+        def tile(name, shape, dtype):
+            return sb.tile(shape, dtype, name=name, align_bytes=64)
+
+        def bank(b, name):
+            return ps.tile([P, BANK], F32, name=name, tag="bank%d" % b)
+
+        offs_sb = tile("offs_sb", [P, SLOTS // 16], U16)
+        offs2_sb = tile("offs2_sb", [P, SLOTS // 16], U16)
+        key_words = tile("key_words", [P, T], U32)
+        val_words = tile("val_words", [P, T], U32)
+        key_scales = tile("key_scales", [P, T], U8)
+        val_scales = tile("val_scales", [P, T], U8)
+        query_raw = tile("query_raw", [P, PACK, Q], F32)
+        gout_raw = tile("gout_raw", [P, PACK, Q], F32)
+        qrows_raw = [tile("qrows_raw%d" % h, [P, PACK, D // 2], F32) for h in range(2)]
+        old_sb = [tile("old_sb%d" % h, [P, PACK, HALF], F32) for h in range(2)]
+        lse_sb = tile("lse_sb", [P, PACK], F32)
+        delta_sb = tile("delta_sb", [P, PACK], F32)
+        qs_sb = tile("qs_sb", [P, PACK], F32)
+        fade_rows = tile("fade_rows", [P, P], F32)
+        ident = tile("ident", [P, P], F32)
+        df = [tile("df%d" % j, [P, U], F32) for j in range(PACK)]
+
+        nc.vector.memset(key_scales[:].bitcast(I32), 0)
+        nc.vector.memset(val_scales[:].bitcast(I32), 0)
+
+        def load_scales(dst, src, row):
+            for quad in range(4):
+                nc.sync.dma_start(dst[32 * quad + row:32 * quad + row + 4, :].bitcast(I32), src[0][4 * quad:4 * quad + 4, :].bitcast(I32))
+
+        def load_words(dst, src):
+            nc.sync.dma_start(dst[:].bitcast(I32), src[0].rearrange("p n t -> p (n t)").bitcast(I32))
+
+        query_view = query.rearrange("(p j) q -> p j q", j=PACK)
+        for h in range(2):
+            nc.sync.dma_start(query_raw[:, 2 * h:2 * h + 2, :], query_view[:, 2 * h:2 * h + 2, :])
+        nc.sync.dma_start(offs_sb[:], offs)
+        load_words(key_words, keys_words)
+        load_scales(key_scales, keys_scales, 0)
+        nc.sync.dma_start(gout_raw[:], gout.rearrange("(p j) q -> p j q", j=PACK))
+        load_scales(val_scales, vals_scales, VAL_ROW)
+        load_words(val_words, vals_words)
+        qrows_view = qrows.rearrange("(p j) d -> p j d", j=PACK)
+        for h in range(2):
+            nc.sync.dma_start(qrows_raw[h][:], qrows_view[:, :, h * (D // 2):(h + 1) * (D // 2)])
+        nc.sync.dma_start(offs2_sb[:], offs2)
+        old_view = old.rearrange("(p j) u -> p j u", j=PACK)
+        for h in range(2):
+            nc.sync.dma_start(old_sb[h][:], old_view[:, :, h * HALF:(h + 1) * HALF])
+        nc.gpsimd.dma_start(lse_sb[:], lse.rearrange("(p r) o -> p (r o)", r=PACK))
+        nc.gpsimd.dma_start(qs_sb[:], qs.rearrange("(p r) o -> p (r o)", r=PACK))
+        nc.gpsimd.dma_start(delta_sb[:], delta.rearrange("(p r) o -> p (r o)", r=PACK))
+        nc.gpsimd.memset(fade_rows[:], 0.0)
+        nc.gpsimd.dma_start(fade_rows[0:U // P, :], fade.rearrange("o (c p) -> (o c) p", p=P))
+        make_identity(nc, ident[:])
+
+        for j in range(PACK):
+            nc.vector.memset(df[j][:], 0.0)
+
+        def quantize(codes, scales, grouped):
+            nc.vector.quantize_mx(out=codes.bitcast(FP8X4), scales=scales, in_=grouped)
+
+        def quantize_dealt(name, raw):
+            grouped = tile(name + "_grouped", [P, PACK, P, PACK], BF16)
+            codes = tile(name + "_codes", [P, Q], U32)
+            scales = tile(name + "_scales", [P, Q], U8)
+            nc.vector.tensor_copy(grouped[:].rearrange("p r m j -> p m j r"), raw[:].rearrange("p j (m r) -> p m j r", r=PACK))
+            quantize(codes[:], scales[:], grouped[:].rearrange("p r m j -> p (r m j)"))
+            return codes, scales
+
+        def gather(name, words, scales, row):
+            picked_scales = tile(name + "_picked_scales", [P, SLOTS], U8)
+            picked_words = tile(name + "_picked_words", [P, SLOTS], U32)
+            nc.vector.tensor_copy(picked_scales[:], scales[:].indirect(offs_sb[:]))
+            nc.vector.tensor_copy(picked_words[:], words[:].indirect(offs_sb[:]))
+            return picked_words[:], picked_scales[row:P, :]
+
+        def product(out, stationary, r, moving):
+            cols = slice(r * P, (r + 1) * P)
+            nc.tensor.matmul_mx(out=out, lhsT=stationary[0][:, cols].bitcast(FP8X4), lhsT_scale=stationary[1][:, cols],
+                                rhs=moving[0].bitcast(FP8X4), rhs_scale=moving[1], start=True, stop=True)
+
+        query_mx = quantize_dealt("query", query_raw)
+        keys_mx = gather("keys", key_words, key_scales, 0)
+        neg_lse = tile("neg_lse", [P, PACK], F32)
+        nc.scalar.mul(neg_lse[:], lse_sb[:], -1.0)
+        weights = tile("weights", [P, PACK, SLOTS], F32)
+        scaled = tile("scaled", [P, PACK, SLOTS], F32)
+        score_banks = [bank(b, "scores%d" % b) for b in range(2)]
+        for r in range(PACK):
+            product(score_banks[r // 2][:, (r % 2) * SLOTS:(r % 2 + 1) * SLOTS], query_mx, r, keys_mx)
+        for r in range(PACK):
+            nc.scalar.activation(weights[:, r, :], score_banks[r // 2][:, (r % 2) * SLOTS:(r % 2 + 1) * SLOTS], ACT.Exp,
+                                 bias=neg_lse[:, r:r + 1])
+        for r in range(PACK):
+            nc.scalar.activation(scaled[:, r, :], weights[:, r, :], ACT.Copy, scale=qs_sb[:, r:r + 1])
+
+        gout_mx = quantize_dealt("gout", gout_raw)
+        vals_mx = gather("vals", val_words, val_scales, VAL_ROW)
+        ds_rows = tile("ds_rows", [P, PACK, SLOTS], BF16)
+        dp_banks = [bank(2 + r, "dp%d" % r) for r in range(PACK)]
+        for r in range(PACK):
+            product(dp_banks[r][:, 0:SLOTS], gout_mx, r, vals_mx)
+        for r in range(PACK):
+            nc.vector.scalar_tensor_tensor(ds_rows[:, r, :], dp_banks[r][:, 0:SLOTS], delta_sb[:, r:r + 1], scaled[:, r, :],
+                                           ALU.subtract, ALU.mult)
+        ds_grouped = tile("ds_grouped", [P, SLOTS, PACK], BF16)
+        nc.vector.tensor_copy(ds_grouped[:].rearrange("p (c i) r -> p c r i", i=4), ds_rows[:].rearrange("p r (c i) -> p c r i", i=4))
+        ds_codes = tile("ds_codes", [P, SLOTS], U32)
+        ds_scales = tile("ds_scales", [P, SLOTS], U8)
+        quantize(ds_codes[:], ds_scales[:], ds_grouped[:].rearrange("p i r -> p (i r)"))
+
+        qrows_grouped = tile("qrows_grouped", [P, PACK, P, PACK], BF16)
+        for h in range(2):
+            nc.scalar.copy(qrows_grouped[:, :, h * (P // 2):(h + 1) * (P // 2), :].rearrange("p t m j -> p m j t"),
+                           qrows_raw[h][:].rearrange("p j (m t) -> p m j t", t=PACK))
+        qrows_codes = tile("qrows_codes", [P, D], U32)
+        qrows_scales = tile("qrows_scales", [P, D], U8)
+        for t0, t1 in ((0, 1), (1, 2), (2, 4)):
+            quantize(qrows_codes[:, t0 * P:t1 * P], qrows_scales[:, t0 * P:t1 * P],
+                     qrows_grouped[:, t0:t1, :, :].rearrange("p t m j -> p (t m j)"))
+
+        fade_bank = bank(6, "fade_bank")
+        nc.tensor.transpose(fade_bank[:, 0:P], fade_rows[:], ident[:])
+        fade_cols = tile("fade_cols", [P, U // P], F32)
+        nc.scalar.copy(fade_cols[:], fade_bank[:, 0:U // P])
+
+        dk_bank_of = (0, 1, 6, 7)
+        dk_banks = [bank(dk_bank_of[j], "dk%d" % j) for j in range(PACK)]
+        dk_sb = [tile("dk_sb%d" % j, [P, SLOTS], F32) for j in range(PACK)]
+        for j in range(PACK):
+            product(dk_banks[j][:, 0:SLOTS], (qrows_codes, qrows_scales), j, (ds_codes[:], ds_scales[:]))
+        for j in range(PACK):
+            nc.scalar.copy(dk_sb[j][:], dk_banks[j][:, 0:SLOTS])
+        for j in range(PACK):
+            nc.vector.tensor_copy(df[j][:].indirect(offs2_sb[:]), dk_sb[j][:])
+
+        faded_t = [tile("faded_t%d" % c, [P, PACK, P], F32) for c in range(U // P)]
+        for c in range(U // P):
+            turned = bank(dk_bank_of[c % 4], "turned%d" % c)
+            for j in range(PACK):
+                nc.tensor.transpose(turned[:, j * P:(j + 1) * P], old_sb[c // 4][:, j, (c % 4) * P:(c % 4 + 1) * P], ident[:])
+            nc.scalar.activation(faded_t[c][:].rearrange("p j m -> p (j m)"), turned[:], ACT.Copy, scale=fade_cols[:, c:c + 1])
+
+        y = [tile("y%d" % h, [P, PACK, HALF], F32) for h in range(2)]
+        out_view = out_0.rearrange("(p j) u -> p j u", j=PACK)
+        for h in range(2):
+            for j in range(PACK):
+                faded = bank(2 + j if h == 0 else dk_bank_of[j], "faded%d_%d" % (h, j))
+                for cc in range(4):
+                    nc.tensor.transpose(faded[:, cc * P:(cc + 1) * P], faded_t[4 * h + cc][:, j, :], ident[:])
+                nc.vector.tensor_tensor(y[h][:, j, :], faded[:], df[j][:, h * HALF:(h + 1) * HALF], ALU.add)
+                if j % 2 == 1:
+                    nc.sync.dma_start(out_view[:, j - 1:j + 1, h * HALF:(h + 1) * HALF], y[h][:, j - 1:j + 1, :])
+
+        y_words = [tile("y_words%d" % h, [P, HALF], U32) for h in range(2)]
+        y_scales = tile("y_scales", [P, U], U8)
+        words_view = out_1[0].rearrange("p n t -> p (n t)").bitcast(I32)
+        y_grouped = [tile("y_grouped%d" % c, [P, QUARTER, PACK], BF16) for c in range(4)]
+
+        def regroup(c, copy):
+            copy(y_grouped[c][:].rearrange("p (n i) j -> p n j i", i=4),
+                 y[c // 2][:, :, (c % 2) * QUARTER:(c % 2 + 1) * QUARTER].rearrange("p j (n i) -> p n j i", i=4))
+
+        def quantize_y(c):
+            quantize(y_words[c // 2][:, (c % 2) * QUARTER:(c % 2 + 1) * QUARTER], y_scales[:, c * QUARTER:(c + 1) * QUARTER],
+                     y_grouped[c][:].rearrange("p n j -> p (n j)"))
+
+        for c in range(3):
+            regroup(c, nc.scalar.copy)
+        quantize_y(0)
+        regroup(3, nc.vector.tensor_copy)
+        quantize_y(1)
+        nc.sync.dma_start(words_view[:, 0:HALF], y_words[0][:].bitcast(I32))
+        quantize_y(3)
+        quantize_y(2)
+        nc.sync.dma_start(words_view[:, HALF:U], y_words[1][:].bitcast(I32))
+        for quad in range(4):
+            nc.scalar.dma_start(out_2[0][4 * quad:4 * quad + 4, :].bitcast(I32), y_scales[32 * quad:32 * quad + 4, :].bitcast(I32))

@@ -31,8 +31,8 @@ def tile_attend_gkeystore_pl_kernel(tc, query, keys_words, keys_scales, gout, va
         sb = ctx.enter_context(tc.tile_pool(name="sb", bufs=1))
         ps = ctx.enter_context(tc.psum_pool(name="ps", bufs=1))
 
-        def tile(name, shape, dtype):
-            return sb.tile(shape, dtype, name=name, align_bytes=64)
+        def tile(name, shape, dtype, tag=None):
+            return sb.tile(shape, dtype, name=name, tag=tag or name, align_bytes=64)
 
         def bank(b, name):
             return ps.tile([P, BANK], F32, name=name, tag="bank%d" % b)
@@ -46,7 +46,8 @@ def tile_attend_gkeystore_pl_kernel(tc, query, keys_words, keys_scales, gout, va
         query_raw = tile("query_raw", [P, PACK, Q], F32)
         gout_raw = tile("gout_raw", [P, PACK, Q], F32)
         qrows_raw = [tile("qrows_raw%d" % h, [P, PACK, D // 2], F32) for h in range(2)]
-        old_sb = [tile("old_sb%d" % h, [P, PACK, HALF], F32) for h in range(2)]
+        old_first = tile("old_first", [P, U], F32)
+        old_rest = [tile("old_rest%d" % h, [P, PACK - 1, HALF], F32) for h in range(2)]
         lse_sb = tile("lse_sb", [P, PACK], F32)
         delta_sb = tile("delta_sb", [P, PACK], F32)
         qs_sb = tile("qs_sb", [P, PACK], F32)
@@ -78,13 +79,14 @@ def tile_attend_gkeystore_pl_kernel(tc, query, keys_words, keys_scales, gout, va
             nc.sync.dma_start(qrows_raw[h][:], qrows_view[:, :, h * (D // 2):(h + 1) * (D // 2)])
         nc.sync.dma_start(offs2_sb[:], offs2)
         old_view = old.rearrange("(p j) u -> p j u", j=PACK)
+        nc.sync.dma_start(old_first[:], old_view[:, 0, :])
         for h in range(2):
-            nc.sync.dma_start(old_sb[h][:], old_view[:, :, h * HALF:(h + 1) * HALF])
-        nc.gpsimd.dma_start(lse_sb[:], lse.rearrange("(p r) o -> p (r o)", r=PACK))
-        nc.gpsimd.dma_start(qs_sb[:], qs.rearrange("(p r) o -> p (r o)", r=PACK))
-        nc.gpsimd.dma_start(delta_sb[:], delta.rearrange("(p r) o -> p (r o)", r=PACK))
+            nc.sync.dma_start(old_rest[h][:], old_view[:, 1:PACK, h * HALF:(h + 1) * HALF])
+        nc.scalar.dma_start(lse_sb[:], lse.rearrange("(p r) o -> p (r o)", r=PACK))
+        nc.scalar.dma_start(qs_sb[:], qs.rearrange("(p r) o -> p (r o)", r=PACK))
+        nc.scalar.dma_start(delta_sb[:], delta.rearrange("(p r) o -> p (r o)", r=PACK))
         nc.gpsimd.memset(fade_rows[:], 0.0)
-        nc.gpsimd.dma_start(fade_rows[0:U // P, :], fade.rearrange("o (c p) -> (o c) p", p=P))
+        nc.scalar.dma_start(fade_rows[0:U // P, :], fade.rearrange("o (c p) -> (o c) p", p=P))
         make_identity(nc, ident[:])
 
         for j in range(PACK):
@@ -93,11 +95,11 @@ def tile_attend_gkeystore_pl_kernel(tc, query, keys_words, keys_scales, gout, va
         def quantize(codes, scales, grouped):
             nc.vector.quantize_mx(out=codes.bitcast(FP8X4), scales=scales, in_=grouped)
 
-        def quantize_dealt(name, raw):
+        def quantize_dealt(name, raw, copy):
             grouped = tile(name + "_grouped", [P, PACK, P, PACK], BF16)
             codes = tile(name + "_codes", [P, Q], U32)
             scales = tile(name + "_scales", [P, Q], U8)
-            nc.vector.tensor_copy(grouped[:].rearrange("p r m j -> p m j r"), raw[:].rearrange("p j (m r) -> p m j r", r=PACK))
+            copy(grouped[:].rearrange("p r m j -> p m j r"), raw[:].rearrange("p j (m r) -> p m j r", r=PACK))
             quantize(codes[:], scales[:], grouped[:].rearrange("p r m j -> p (r m j)"))
             return codes, scales
 
@@ -113,7 +115,7 @@ def tile_attend_gkeystore_pl_kernel(tc, query, keys_words, keys_scales, gout, va
             nc.tensor.matmul_mx(out=out, lhsT=stationary[0][:, cols].bitcast(FP8X4), lhsT_scale=stationary[1][:, cols],
                                 rhs=moving[0].bitcast(FP8X4), rhs_scale=moving[1], start=True, stop=True)
 
-        query_mx = quantize_dealt("query", query_raw)
+        query_mx = quantize_dealt("query", query_raw, nc.scalar.copy)
         keys_mx = gather("keys", key_words, key_scales, 0)
         neg_lse = tile("neg_lse", [P, PACK], F32)
         nc.scalar.mul(neg_lse[:], lse_sb[:], -1.0)
@@ -128,7 +130,7 @@ def tile_attend_gkeystore_pl_kernel(tc, query, keys_words, keys_scales, gout, va
         for r in range(PACK):
             nc.scalar.activation(scaled[:, r, :], weights[:, r, :], ACT.Copy, scale=qs_sb[:, r:r + 1])
 
-        gout_mx = quantize_dealt("gout", gout_raw)
+        gout_mx = quantize_dealt("gout", gout_raw, nc.vector.tensor_copy)
         vals_mx = gather("vals", val_words, val_scales, VAL_ROW)
         ds_rows = tile("ds_rows", [P, PACK, SLOTS], BF16)
         dp_banks = [bank(2 + r, "dp%d" % r) for r in range(PACK)]
@@ -157,9 +159,11 @@ def tile_attend_gkeystore_pl_kernel(tc, query, keys_words, keys_scales, gout, va
         nc.tensor.transpose(fade_bank[:, 0:P], fade_rows[:], ident[:])
         fade_cols = tile("fade_cols", [P, U // P], F32)
         nc.scalar.copy(fade_cols[:], fade_bank[:, 0:U // P])
+        fade_wide = [bank(6 + h, "fade_wide%d" % h) for h in range(2)]
+        for c in range(U // P):
+            nc.tensor.transpose(fade_wide[c // 4][:, (c % 4) * P:(c % 4 + 1) * P], fade_cols[:, c:c + 1].to_broadcast([P, P]), ident[:])
 
-        dk_bank_of = (0, 1, 6, 7)
-        dk_banks = [bank(dk_bank_of[j], "dk%d" % j) for j in range(PACK)]
+        dk_banks = [bank(j, "dk%d" % j) for j in range(PACK)]
         dk_sb = [tile("dk_sb%d" % j, [P, SLOTS], F32) for j in range(PACK)]
         for j in range(PACK):
             product(dk_banks[j][:, 0:SLOTS], (qrows_codes, qrows_scales), j, (ds_codes[:], ds_scales[:]))
@@ -168,23 +172,30 @@ def tile_attend_gkeystore_pl_kernel(tc, query, keys_words, keys_scales, gout, va
         for j in range(PACK):
             nc.vector.tensor_copy(df[j][:].indirect(offs2_sb[:]), dk_sb[j][:])
 
-        faded_t = [tile("faded_t%d" % c, [P, PACK, P], F32) for c in range(U // P)]
+        faded_first = tile("faded_first", [P, U], F32)
+        for h in range(2):
+            nc.vector.tensor_tensor(faded_first[:, h * HALF:(h + 1) * HALF], fade_wide[h][:], old_first[:, h * HALF:(h + 1) * HALF], ALU.mult)
+
+        faded_t = [tile("faded_t%d" % c, [P, PACK - 1, P], F32) for c in range(U // P)]
         for c in range(U // P):
-            turned = bank(dk_bank_of[c % 4], "turned%d" % c)
-            for j in range(PACK):
-                nc.tensor.transpose(turned[:, j * P:(j + 1) * P], old_sb[c // 4][:, j, (c % 4) * P:(c % 4 + 1) * P], ident[:])
-            nc.scalar.activation(faded_t[c][:].rearrange("p j m -> p (j m)"), turned[:], ACT.Copy, scale=fade_cols[:, c:c + 1])
+            turned = bank((4, 5, 0, 1)[c % 4], "turned%d" % c)
+            for j in range(PACK - 1):
+                nc.tensor.transpose(turned[:, j * P:(j + 1) * P], old_rest[c // 4][:, j, (c % 4) * P:(c % 4 + 1) * P], ident[:])
+            nc.scalar.activation(faded_t[c][:].rearrange("p j m -> p (j m)"), turned[:, 0:(PACK - 1) * P], ACT.Copy,
+                                 scale=fade_cols[:, c:c + 1])
 
         y = [tile("y%d" % h, [P, PACK, HALF], F32) for h in range(2)]
         out_view = out_0.rearrange("(p j) u -> p j u", j=PACK)
         for h in range(2):
-            for j in range(PACK):
-                faded = bank(2 + j if h == 0 else dk_bank_of[j], "faded%d_%d" % (h, j))
+            cols = slice(h * HALF, (h + 1) * HALF)
+            nc.vector.tensor_tensor(y[h][:, 0, :], faded_first[:, cols], df[0][:, cols], ALU.add)
+            for j in range(1, PACK):
+                faded = bank(((6, 7, 2), (3, 4, 5))[h][j - 1], "faded%d_%d" % (h, j))
                 for cc in range(4):
-                    nc.tensor.transpose(faded[:, cc * P:(cc + 1) * P], faded_t[4 * h + cc][:, j, :], ident[:])
-                nc.vector.tensor_tensor(y[h][:, j, :], faded[:], df[j][:, h * HALF:(h + 1) * HALF], ALU.add)
+                    nc.tensor.transpose(faded[:, cc * P:(cc + 1) * P], faded_t[4 * h + cc][:, j - 1, :], ident[:])
+                nc.vector.tensor_tensor(y[h][:, j, :], faded[:], df[j][:, cols], ALU.add)
                 if j % 2 == 1:
-                    nc.sync.dma_start(out_view[:, j - 1:j + 1, h * HALF:(h + 1) * HALF], y[h][:, j - 1:j + 1, :])
+                    nc.sync.dma_start(out_view[:, j - 1:j + 1, cols], y[h][:, j - 1:j + 1, :])
 
         y_words = [tile("y_words%d" % h, [P, HALF], U32) for h in range(2)]
         y_scales = tile("y_scales", [P, U], U8)

@@ -95,90 +95,101 @@ def tile_attend_gkeystore_pl_kernel(tc, query, keys_words, keys_scales, gout, va
         def quantize(codes, scales, grouped):
             nc.vector.quantize_mx(out=codes.bitcast(FP8X4), scales=scales, in_=grouped)
 
-        def quantize_dealt(name, raw, copy):
+        def deal(name, raw, copy):
             grouped = tile(name + "_grouped", [P, PACK, P, PACK], BF16)
+            copy(grouped[:].rearrange("p r m j -> p m j r"), raw[:].rearrange("p j (m r) -> p m j r", r=PACK))
+            return grouped
+
+        def quantize_dealt(name, grouped):
             codes = tile(name + "_codes", [P, Q], U32)
             scales = tile(name + "_scales", [P, Q], U8)
-            copy(grouped[:].rearrange("p r m j -> p m j r"), raw[:].rearrange("p j (m r) -> p m j r", r=PACK))
             quantize(codes[:], scales[:], grouped[:].rearrange("p r m j -> p (r m j)"))
-            return codes, scales
+            return [(codes[:, r * P:(r + 1) * P], scales[:, r * P:(r + 1) * P]) for r in range(PACK)]
 
-        def gather(name, words, scales, row):
-            picked_scales = tile(name + "_picked_scales", [P, SLOTS], U8)
-            picked_words = tile(name + "_picked_words", [P, SLOTS], U32)
-            nc.vector.tensor_copy(picked_scales[:], scales[:].indirect(offs_sb[:]))
-            nc.vector.tensor_copy(picked_words[:], words[:].indirect(offs_sb[:]))
-            return picked_words[:], picked_scales[row:P, :]
+        def gather(name, window, dtype):
+            picked = tile(name, [P, SLOTS], dtype)
+            nc.vector.tensor_copy(picked[:], window[:].indirect(offs_sb[:]))
+            return picked
 
-        def product(out, stationary, r, moving):
-            cols = slice(r * P, (r + 1) * P)
-            nc.tensor.matmul_mx(out=out, lhsT=stationary[0][:, cols].bitcast(FP8X4), lhsT_scale=stationary[1][:, cols],
+        def product(out, stationary, moving):
+            nc.tensor.matmul_mx(out=out, lhsT=stationary[0].bitcast(FP8X4), lhsT_scale=stationary[1],
                                 rhs=moving[0].bitcast(FP8X4), rhs_scale=moving[1], start=True, stop=True)
 
-        query_mx = quantize_dealt("query", query_raw, nc.scalar.copy)
-        keys_mx = gather("keys", key_words, key_scales, 0)
+        query_grouped = deal("query", query_raw, nc.scalar.copy)
+        keys_mx = (gather("picked_key_words", key_words, U32)[:], gather("picked_key_scales", key_scales, U8)[:])
+        query_mx = quantize_dealt("query", query_grouped)
         neg_lse = tile("neg_lse", [P, PACK], F32)
         nc.scalar.mul(neg_lse[:], lse_sb[:], -1.0)
         weights = tile("weights", [P, PACK, SLOTS], F32)
         scaled = tile("scaled", [P, PACK, SLOTS], F32)
         score_banks = [bank(b, "scores%d" % b) for b in range(2)]
         for r in range(PACK):
-            product(score_banks[r // 2][:, (r % 2) * SLOTS:(r % 2 + 1) * SLOTS], query_mx, r, keys_mx)
+            product(score_banks[r // 2][:, (r % 2) * SLOTS:(r % 2 + 1) * SLOTS], query_mx[r], keys_mx)
         for r in range(PACK):
             nc.scalar.activation(weights[:, r, :], score_banks[r // 2][:, (r % 2) * SLOTS:(r % 2 + 1) * SLOTS], ACT.Exp,
                                  bias=neg_lse[:, r:r + 1])
         for r in range(PACK):
             nc.scalar.activation(scaled[:, r, :], weights[:, r, :], ACT.Copy, scale=qs_sb[:, r:r + 1])
 
-        gout_mx = quantize_dealt("gout", gout_raw, nc.vector.tensor_copy)
-        vals_mx = gather("vals", val_words, val_scales, VAL_ROW)
+        gout_grouped = deal("gout", gout_raw, nc.vector.tensor_copy)
+        picked_val_scales = gather("picked_val_scales", val_scales, U8)
+        gout_mx = quantize_dealt("gout", gout_grouped)
+        vals_mx = (gather("picked_val_words", val_words, U32)[:], picked_val_scales[VAL_ROW:P, :])
         ds_rows = tile("ds_rows", [P, PACK, SLOTS], BF16)
         dp_banks = [bank(2 + r, "dp%d" % r) for r in range(PACK)]
         for r in range(PACK):
-            product(dp_banks[r][:, 0:SLOTS], gout_mx, r, vals_mx)
+            product(dp_banks[r][:, 0:SLOTS], gout_mx[r], vals_mx)
         for r in range(PACK):
             nc.vector.scalar_tensor_tensor(ds_rows[:, r, :], dp_banks[r][:, 0:SLOTS], delta_sb[:, r:r + 1], scaled[:, r, :],
                                            ALU.subtract, ALU.mult)
-        ds_grouped = tile("ds_grouped", [P, SLOTS, PACK], BF16)
-        nc.vector.tensor_copy(ds_grouped[:].rearrange("p (c i) r -> p c r i", i=4), ds_rows[:].rearrange("p r (c i) -> p c r i", i=4))
+        ds_grouped = tile("ds_grouped", [P, SLOTS * PACK], BF16)
+        nc.vector.tensor_copy(ds_grouped[:].rearrange("p (c i r) -> p c r i", i=4, r=PACK), ds_rows[:].rearrange("p r (c i) -> p c r i", i=4))
         ds_codes = tile("ds_codes", [P, SLOTS], U32)
         ds_scales = tile("ds_scales", [P, SLOTS], U8)
-        quantize(ds_codes[:], ds_scales[:], ds_grouped[:].rearrange("p i r -> p (i r)"))
+        quantize(ds_codes[:], ds_scales[:], ds_grouped[:])
 
         qrows_grouped = tile("qrows_grouped", [P, PACK, P, PACK], BF16)
         for h in range(2):
             nc.scalar.copy(qrows_grouped[:, :, h * (P // 2):(h + 1) * (P // 2), :].rearrange("p t m j -> p m j t"),
                            qrows_raw[h][:].rearrange("p j (m t) -> p m j t", t=PACK))
-        qrows_codes = tile("qrows_codes", [P, D], U32)
+        first_codes = tile("first_codes", [P, P], U32)
+        rest_codes = tile("rest_codes", [P, D - P], U32, tag="ds_grouped")
         qrows_scales = tile("qrows_scales", [P, D], U8)
-        for t0, t1 in ((0, 1), (1, 2), (2, 4)):
-            quantize(qrows_codes[:, t0 * P:t1 * P], qrows_scales[:, t0 * P:t1 * P],
+        quantize(first_codes[:], qrows_scales[:, 0:P], qrows_grouped[:, 0, :, :].rearrange("p m j -> p (m j)"))
+        for t0, t1 in ((1, 2), (2, 4)):
+            quantize(rest_codes[:, (t0 - 1) * P:(t1 - 1) * P], qrows_scales[:, t0 * P:t1 * P],
                      qrows_grouped[:, t0:t1, :, :].rearrange("p t m j -> p (t m j)"))
+        qrows_mx = [(first_codes[:] if j == 0 else rest_codes[:, (j - 1) * P:j * P], qrows_scales[:, j * P:(j + 1) * P])
+                    for j in range(PACK)]
 
         fade_bank = bank(6, "fade_bank")
         nc.tensor.transpose(fade_bank[:, 0:P], fade_rows[:], ident[:])
         fade_cols = tile("fade_cols", [P, U // P], F32)
         nc.scalar.copy(fade_cols[:], fade_bank[:, 0:U // P])
-        fade_wide = [bank(6 + h, "fade_wide%d" % h) for h in range(2)]
-        for c in range(U // P):
-            nc.tensor.transpose(fade_wide[c // 4][:, (c % 4) * P:(c % 4 + 1) * P], fade_cols[:, c:c + 1].to_broadcast([P, P]), ident[:])
+        fade_wide = tile("fade_wide", [P, U], F32)
+        for h in range(2):
+            spread = bank(7 - h, "spread%d" % h)
+            for cc in range(4):
+                c = 4 * h + cc
+                nc.tensor.transpose(spread[:, cc * P:(cc + 1) * P], fade_cols[:, c:c + 1].to_broadcast([P, P]), ident[:])
+            nc.scalar.copy(fade_wide[:, h * HALF:(h + 1) * HALF], spread[:])
 
         dk_banks = [bank(j, "dk%d" % j) for j in range(PACK)]
         dk_sb = [tile("dk_sb%d" % j, [P, SLOTS], F32) for j in range(PACK)]
         for j in range(PACK):
-            product(dk_banks[j][:, 0:SLOTS], (qrows_codes, qrows_scales), j, (ds_codes[:], ds_scales[:]))
+            product(dk_banks[j][:, 0:SLOTS], qrows_mx[j], (ds_codes[:], ds_scales[:]))
         for j in range(PACK):
             nc.scalar.copy(dk_sb[j][:], dk_banks[j][:, 0:SLOTS])
         for j in range(PACK):
             nc.vector.tensor_copy(df[j][:].indirect(offs2_sb[:]), dk_sb[j][:])
 
-        faded_first = tile("faded_first", [P, U], F32)
+        faded_first = tile("faded_first", [P, U], F32, tag="qrows_grouped")
         for h in range(2):
-            nc.vector.tensor_tensor(faded_first[:, h * HALF:(h + 1) * HALF], fade_wide[h][:], old_first[:, h * HALF:(h + 1) * HALF], ALU.mult)
+            nc.gpsimd.tensor_tensor(faded_first[:, h * HALF:(h + 1) * HALF], fade_wide[:, h * HALF:(h + 1) * HALF], old_first[:, h * HALF:(h + 1) * HALF], ALU.mult)
 
         faded_t = [tile("faded_t%d" % c, [P, PACK - 1, P], F32) for c in range(U // P)]
         for c in range(U // P):
-            turned = bank((4, 5, 0, 1)[c % 4], "turned%d" % c)
+            turned = bank(c % 4, "turned%d" % c)
             for j in range(PACK - 1):
                 nc.tensor.transpose(turned[:, j * P:(j + 1) * P], old_rest[c // 4][:, j, (c % 4) * P:(c % 4 + 1) * P], ident[:])
             nc.scalar.activation(faded_t[c][:].rearrange("p j m -> p (j m)"), turned[:, 0:(PACK - 1) * P], ACT.Copy,
@@ -186,38 +197,53 @@ def tile_attend_gkeystore_pl_kernel(tc, query, keys_words, keys_scales, gout, va
 
         y = [tile("y%d" % h, [P, PACK, HALF], F32) for h in range(2)]
         out_view = out_0.rearrange("(p j) u -> p j u", j=PACK)
+        faded_banks = {}
+        faded_second = [tile("faded_second%d" % h, [P, HALF], F32) for h in range(2)]
+        for h in range(2):
+            for j in range(1, PACK):
+                faded_banks[h, j] = bank(((4, 5, 6), (7, 0, 1))[h][j - 1], "faded%d_%d" % (h, j))
+                for cc in range(4):
+                    nc.tensor.transpose(faded_banks[h, j][:, cc * P:(cc + 1) * P], faded_t[4 * h + cc][:, j - 1, :], ident[:])
+            nc.scalar.copy(faded_second[h][:], faded_banks[h, 1][:])
         for h in range(2):
             cols = slice(h * HALF, (h + 1) * HALF)
-            nc.vector.tensor_tensor(y[h][:, 0, :], faded_first[:, cols], df[0][:, cols], ALU.add)
-            for j in range(1, PACK):
-                faded = bank(((6, 7, 2), (3, 4, 5))[h][j - 1], "faded%d_%d" % (h, j))
-                for cc in range(4):
-                    nc.tensor.transpose(faded[:, cc * P:(cc + 1) * P], faded_t[4 * h + cc][:, j - 1, :], ident[:])
-                nc.vector.tensor_tensor(y[h][:, j, :], faded[:], df[j][:, cols], ALU.add)
-                if j % 2 == 1:
-                    nc.sync.dma_start(out_view[:, j - 1:j + 1, cols], y[h][:, j - 1:j + 1, :])
+            nc.gpsimd.tensor_tensor(y[h][:, 0, :], faded_first[:, cols], df[0][:, cols], ALU.add)
+        for h in range(2):
+            cols = slice(h * HALF, (h + 1) * HALF)
+            nc.gpsimd.tensor_tensor(y[h][:, 1, :], faded_second[h][:], df[1][:, cols], ALU.add)
+            nc.sync.dma_start(out_view[:, 0:2, cols], y[h][:, 0:2, :])
+        for h, pieces in ((0, ((0, QUARTER), (QUARTER, HALF))), (1, ((0, HALF),))):
+            for n0, n1 in pieces:
+                for j in range(2, PACK):
+                    nc.vector.tensor_tensor(y[h][:, j, n0:n1], faded_banks[h, j][:, n0:n1], df[j][:, h * HALF + n0:h * HALF + n1], ALU.add)
+            nc.sync.dma_start(out_view[:, 2:PACK, h * HALF:(h + 1) * HALF], y[h][:, 2:PACK, :])
 
-        y_words = [tile("y_words%d" % h, [P, HALF], U32) for h in range(2)]
         y_scales = tile("y_scales", [P, U], U8)
         words_view = out_1[0].rearrange("p n t -> p (n t)").bitcast(I32)
-        y_grouped = [tile("y_grouped%d" % c, [P, QUARTER, PACK], BF16) for c in range(4)]
+        y_words = tile("y_words", [P, U], U32)
+        y_grouped = [tile("y_grouped%d" % c, [P, QUARTER, PACK], BF16, tag="faded_t7" if c == 0 else None) for c in range(4)]
 
         def regroup(c, copy):
             copy(y_grouped[c][:].rearrange("p (n i) j -> p n j i", i=4),
                  y[c // 2][:, :, (c % 2) * QUARTER:(c % 2 + 1) * QUARTER].rearrange("p j (n i) -> p n j i", i=4))
 
         def quantize_y(c):
-            quantize(y_words[c // 2][:, (c % 2) * QUARTER:(c % 2 + 1) * QUARTER], y_scales[:, c * QUARTER:(c + 1) * QUARTER],
+            quantize(y_words[:, c * QUARTER:(c + 1) * QUARTER], y_scales[:, c * QUARTER:(c + 1) * QUARTER],
                      y_grouped[c][:].rearrange("p n j -> p (n j)"))
+
+        def store_words(c0, c1):
+            nc.sync.dma_start(words_view[:, c0 * QUARTER:c1 * QUARTER], y_words[:, c0 * QUARTER:c1 * QUARTER].bitcast(I32))
 
         for c in range(3):
             regroup(c, nc.scalar.copy)
-        quantize_y(0)
         regroup(3, nc.vector.tensor_copy)
+        quantize_y(0)
         quantize_y(1)
-        nc.sync.dma_start(words_view[:, 0:HALF], y_words[0][:].bitcast(I32))
+        store_words(0, 2)
         quantize_y(3)
+        store_words(3, 4)
         quantize_y(2)
-        nc.sync.dma_start(words_view[:, HALF:U], y_words[1][:].bitcast(I32))
+        store_words(2, 3)
         for quad in range(4):
-            nc.scalar.dma_start(out_2[0][4 * quad:4 * quad + 4, :].bitcast(I32), y_scales[32 * quad:32 * quad + 4, :].bitcast(I32))
+            queue = nc.sync if quad == 0 else nc.scalar
+            queue.dma_start(out_2[0][4 * quad:4 * quad + 4, :].bitcast(I32), y_scales[32 * quad:32 * quad + 4, :].bitcast(I32))

@@ -45,7 +45,7 @@ def tile_attend_gkeystore_pl_kernel(tc, query, keys_words, keys_scales, gout, va
         val_scales = tile("val_scales", [P, T], U8)
         query_raw = tile("query_raw", [P, PACK, Q], F32)
         gout_raw = tile("gout_raw", [P, PACK, Q], F32)
-        qrows_raw = [tile("qrows_raw%d" % h, [P, PACK, D // 2], F32) for h in range(2)]
+        qrows_raw = tile("qrows_raw", [P, PACK, D], F32)
         old_first = tile("old_first", [P, U], F32)
         old_rest = [tile("old_rest%d" % h, [P, PACK - 1, HALF], F32) for h in range(2)]
         lse_sb = tile("lse_sb", [P, PACK], F32)
@@ -59,8 +59,8 @@ def tile_attend_gkeystore_pl_kernel(tc, query, keys_words, keys_scales, gout, va
         nc.vector.memset(val_scales[:].bitcast(I32), 0)
 
         def load_scales(dst, src, row):
-            for quad in range(4):
-                nc.sync.dma_start(dst[32 * quad + row:32 * quad + row + 4, :].bitcast(I32), src[0][4 * quad:4 * quad + 4, :].bitcast(I32))
+            for r in range(4):
+                nc.sync.dma_start(dst[row + r:P:32, :].bitcast(I32), src[0][r:16:4, :].bitcast(I32))
 
         def load_words(dst, src):
             nc.sync.dma_start(dst[:].bitcast(I32), src[0].rearrange("p n t -> p (n t)").bitcast(I32))
@@ -74,9 +74,7 @@ def tile_attend_gkeystore_pl_kernel(tc, query, keys_words, keys_scales, gout, va
         nc.sync.dma_start(gout_raw[:], gout.rearrange("(p j) q -> p j q", j=PACK))
         load_scales(val_scales, vals_scales, VAL_ROW)
         load_words(val_words, vals_words)
-        qrows_view = qrows.rearrange("(p j) d -> p j d", j=PACK)
-        for h in range(2):
-            nc.sync.dma_start(qrows_raw[h][:], qrows_view[:, :, h * (D // 2):(h + 1) * (D // 2)])
+        nc.sync.dma_start(qrows_raw[:], qrows.rearrange("(p j) d -> p j d", j=PACK))
         nc.sync.dma_start(offs2_sb[:], offs2)
         old_view = old.rearrange("(p j) u -> p j u", j=PACK)
         nc.sync.dma_start(old_first[:], old_view[:, 0, :])
@@ -97,7 +95,7 @@ def tile_attend_gkeystore_pl_kernel(tc, query, keys_words, keys_scales, gout, va
 
         def deal(name, raw, copy):
             grouped = tile(name + "_grouped", [P, PACK, P, PACK], BF16)
-            copy(grouped[:].rearrange("p r m j -> p m j r"), raw[:].rearrange("p j (m r) -> p m j r", r=PACK))
+            copy(grouped[:].rearrange("p (a b) m j -> p a m j b", b=2), raw[:].rearrange("p j (m a b) -> p a m j b", a=2, b=2))
             return grouped
 
         def quantize_dealt(name, grouped):
@@ -143,24 +141,26 @@ def tile_attend_gkeystore_pl_kernel(tc, query, keys_words, keys_scales, gout, va
             nc.vector.scalar_tensor_tensor(ds_rows[:, r, :], dp_banks[r][:, 0:SLOTS], delta_sb[:, r:r + 1], scaled[:, r, :],
                                            ALU.subtract, ALU.mult)
         ds_grouped = tile("ds_grouped", [P, SLOTS * PACK], BF16)
-        nc.vector.tensor_copy(ds_grouped[:].rearrange("p (c i r) -> p c r i", i=4, r=PACK), ds_rows[:].rearrange("p r (c i) -> p c r i", i=4))
         ds_codes = tile("ds_codes", [P, SLOTS], U32)
         ds_scales = tile("ds_scales", [P, SLOTS], U8)
-        quantize(ds_codes[:], ds_scales[:], ds_grouped[:])
+        for g in range(2):
+            nc.vector.tensor_copy(ds_grouped[:, g * P * PACK:(g + 1) * P * PACK].rearrange("p (c i r) -> p c r i", i=2, r=PACK),
+                                  ds_rows[:, :, g * P:(g + 1) * P].rearrange("p r (c i) -> p c r i", i=2))
+        for g in range(2):
+            quantize(ds_codes[:, g * P:(g + 1) * P], ds_scales[:, g * P:(g + 1) * P], ds_grouped[:, g * P * PACK:(g + 1) * P * PACK])
 
         qrows_grouped = tile("qrows_grouped", [P, PACK, P, PACK], BF16)
-        for h in range(2):
-            nc.scalar.copy(qrows_grouped[:, :, h * (P // 2):(h + 1) * (P // 2), :].rearrange("p t m j -> p m j t"),
-                           qrows_raw[h][:].rearrange("p j (m t) -> p m j t", t=PACK))
+        for a in range(2):
+            nc.scalar.copy(qrows_grouped[:, 2 * a:2 * a + 2, :, :].rearrange("p b m j -> p m j b"),
+                           qrows_raw[:].rearrange("p j (m t) -> p m j t", t=PACK)[:, :, :, 2 * a:2 * a + 2])
         first_codes = tile("first_codes", [P, P], U32)
         rest_codes = tile("rest_codes", [P, D - P], U32, tag="ds_grouped")
         qrows_scales = tile("qrows_scales", [P, D], U8)
-        quantize(first_codes[:], qrows_scales[:, 0:P], qrows_grouped[:, 0, :, :].rearrange("p m j -> p (m j)"))
-        for t0, t1 in ((1, 2), (2, 4)):
-            quantize(rest_codes[:, (t0 - 1) * P:(t1 - 1) * P], qrows_scales[:, t0 * P:t1 * P],
-                     qrows_grouped[:, t0:t1, :, :].rearrange("p t m j -> p (t m j)"))
-        qrows_mx = [(first_codes[:] if j == 0 else rest_codes[:, (j - 1) * P:j * P], qrows_scales[:, j * P:(j + 1) * P])
-                    for j in range(PACK)]
+        quantize(first_codes[:], qrows_scales[:, P:2 * P], qrows_grouped[:, 1, :, :].rearrange("p m j -> p (m j)"))
+        quantize(rest_codes[:, 0:P], qrows_scales[:, 0:P], qrows_grouped[:, 0, :, :].rearrange("p m j -> p (m j)"))
+        quantize(rest_codes[:, P:3 * P], qrows_scales[:, 2 * P:4 * P], qrows_grouped[:, 2:4, :, :].rearrange("p t m j -> p (t m j)"))
+        qrows_codes = (rest_codes[:, 0:P], first_codes[:], rest_codes[:, P:2 * P], rest_codes[:, 2 * P:3 * P])
+        qrows_mx = [(qrows_codes[j], qrows_scales[:, j * P:(j + 1) * P]) for j in range(PACK)]
 
         fade_bank = bank(6, "fade_bank")
         nc.tensor.transpose(fade_bank[:, 0:P], fade_rows[:], ident[:])
@@ -174,14 +174,15 @@ def tile_attend_gkeystore_pl_kernel(tc, query, keys_words, keys_scales, gout, va
                 nc.tensor.transpose(spread[:, cc * P:(cc + 1) * P], fade_cols[:, c:c + 1].to_broadcast([P, P]), ident[:])
             nc.scalar.copy(fade_wide[:, h * HALF:(h + 1) * HALF], spread[:])
 
-        dk_banks = [bank(j, "dk%d" % j) for j in range(PACK)]
-        dk_sb = [tile("dk_sb%d" % j, [P, SLOTS], F32) for j in range(PACK)]
-        for j in range(PACK):
-            product(dk_banks[j][:, 0:SLOTS], qrows_mx[j], (ds_codes[:], ds_scales[:]))
-        for j in range(PACK):
-            nc.scalar.copy(dk_sb[j][:], dk_banks[j][:, 0:SLOTS])
-        for j in range(PACK):
-            nc.vector.tensor_copy(df[j][:].indirect(offs2_sb[:]), dk_sb[j][:])
+        pieces = [(1, 0, P, 4), (0, 0, SLOTS, 0), (1, P, SLOTS, 1), (2, 0, SLOTS, 2), (3, 0, SLOTS, 3)]
+        dk_banks = [bank(b, "dk%d_%d" % (j, n0)) for j, n0, n1, b in pieces]
+        dk_sb = [tile("dk_sb%d_%d" % (j, n0), [P, n1 - n0], F32) for j, n0, n1, b in pieces]
+        for k, (j, n0, n1, b) in enumerate(pieces):
+            product(dk_banks[k][:, 0:n1 - n0], qrows_mx[j], (ds_codes[:, n0:n1], ds_scales[:, n0:n1]))
+        for k, (j, n0, n1, b) in enumerate(pieces):
+            nc.scalar.copy(dk_sb[k][:], dk_banks[k][:, 0:n1 - n0])
+        for k, (j, n0, n1, b) in enumerate(pieces):
+            nc.vector.tensor_copy(df[j][:].indirect(offs2_sb[:, n0 // 16:n1 // 16]), dk_sb[k][:])
 
         faded_first = tile("faded_first", [P, U], F32, tag="qrows_grouped")
         for h in range(2):
@@ -208,15 +209,15 @@ def tile_attend_gkeystore_pl_kernel(tc, query, keys_words, keys_scales, gout, va
         for h in range(2):
             cols = slice(h * HALF, (h + 1) * HALF)
             nc.gpsimd.tensor_tensor(y[h][:, 0, :], faded_first[:, cols], df[0][:, cols], ALU.add)
+            nc.sync.dma_start(out_view[:, 0, cols], y[h][:, 0, :])
         for h in range(2):
-            cols = slice(h * HALF, (h + 1) * HALF)
-            nc.gpsimd.tensor_tensor(y[h][:, 1, :], faded_second[h][:], df[1][:, cols], ALU.add)
-            nc.sync.dma_start(out_view[:, 0:2, cols], y[h][:, 0:2, :])
+            nc.gpsimd.tensor_tensor(y[h][:, 1, :], faded_second[h][:], df[1][:, h * HALF:(h + 1) * HALF], ALU.add)
+        nc.sync.dma_start(out_view[:, 1, 0:HALF], y[0][:, 1, :])
         for h, pieces in ((0, ((0, QUARTER), (QUARTER, HALF))), (1, ((0, HALF),))):
             for n0, n1 in pieces:
                 for j in range(2, PACK):
                     nc.vector.tensor_tensor(y[h][:, j, n0:n1], faded_banks[h, j][:, n0:n1], df[j][:, h * HALF + n0:h * HALF + n1], ALU.add)
-            nc.sync.dma_start(out_view[:, 2:PACK, h * HALF:(h + 1) * HALF], y[h][:, 2:PACK, :])
+            nc.sync.dma_start(out_view[:, 2 - h:PACK, h * HALF:(h + 1) * HALF], y[h][:, 2 - h:PACK, :])
 
         y_scales = tile("y_scales", [P, U], U8)
         words_view = out_1[0].rearrange("p n t -> p (n t)").bitcast(I32)
@@ -224,8 +225,8 @@ def tile_attend_gkeystore_pl_kernel(tc, query, keys_words, keys_scales, gout, va
         y_grouped = [tile("y_grouped%d" % c, [P, QUARTER, PACK], BF16, tag="faded_t7" if c == 0 else None) for c in range(4)]
 
         def regroup(c, copy):
-            copy(y_grouped[c][:].rearrange("p (n i) j -> p n j i", i=4),
-                 y[c // 2][:, :, (c % 2) * QUARTER:(c % 2 + 1) * QUARTER].rearrange("p j (n i) -> p n j i", i=4))
+            copy(y_grouped[c][:].rearrange("p (n i) j -> p n j i", i=2),
+                 y[c // 2][:, :, (c % 2) * QUARTER:(c % 2 + 1) * QUARTER].rearrange("p j (n i) -> p n j i", i=2))
 
         def quantize_y(c):
             quantize(y_words[:, c * QUARTER:(c + 1) * QUARTER], y_scales[:, c * QUARTER:(c + 1) * QUARTER],
@@ -244,6 +245,6 @@ def tile_attend_gkeystore_pl_kernel(tc, query, keys_words, keys_scales, gout, va
         store_words(3, 4)
         quantize_y(2)
         store_words(2, 3)
-        for quad in range(4):
-            queue = nc.sync if quad == 0 else nc.scalar
-            queue.dma_start(out_2[0][4 * quad:4 * quad + 4, :].bitcast(I32), y_scales[32 * quad:32 * quad + 4, :].bitcast(I32))
+        for r in range(4):
+            queue = nc.sync if r == 0 else nc.scalar
+            queue.dma_start(out_2[0][r:16:4, :].bitcast(I32), y_scales[r:P:32, :].bitcast(I32))

@@ -16,10 +16,16 @@ ACT = mybir.ActivationFunctionType
 P = 128
 PACK = 4
 D, E, T, SLOTS, U, Q = 512, 512, 2048, 256, 1024, 512
+BANK = 512
 HALF = U // 2
 QUARTER = U // 4
-BANK = 512
+CHUNKS = U // P
+CHUNKS_A_BANK = BANK // P
+LIST_ROWS = 16
+QUADRANT = 32
+SCALE_ROWS = 16
 VAL_ROW = 4
+GPSIMD_PLANES = 2
 
 FLOPS = 2 * Q * SLOTS * (D + E + D)
 
@@ -37,8 +43,14 @@ def tile_attend_gkeystore_pl_kernel(tc, query, keys_words, keys_scales, gout, va
         def bank(b, name):
             return ps.tile([P, BANK], F32, name=name, tag="bank%d" % b)
 
-        offs_sb = tile("offs_sb", [P, SLOTS // 16], U16)
-        offs2_sb = tile("offs2_sb", [P, SLOTS // 16], U16)
+        def half(h):
+            return slice(h * HALF, (h + 1) * HALF)
+
+        def block(n):
+            return slice(n * P, (n + 1) * P)
+
+        offs_sb = tile("offs_sb", [P, SLOTS // LIST_ROWS], U16)
+        offs2_sb = tile("offs2_sb", [P, SLOTS // LIST_ROWS], U16)
         key_words = tile("key_words", [P, T], U32)
         val_words = tile("val_words", [P, T], U32)
         key_scales = tile("key_scales", [P, T], U8)
@@ -58,33 +70,37 @@ def tile_attend_gkeystore_pl_kernel(tc, query, keys_words, keys_scales, gout, va
         nc.vector.memset(key_scales[:].bitcast(I32), 0)
         nc.vector.memset(val_scales[:].bitcast(I32), 0)
 
-        def load_scales(dst, src, row):
+        def load_scales(dst, src, first):
             for r in range(4):
-                nc.sync.dma_start(dst[row + r:P:32, :].bitcast(I32), src[0][r:16:4, :].bitcast(I32))
+                nc.sync.dma_start(dst[first + r:P:QUADRANT, :].bitcast(I32), src[0][r:SCALE_ROWS:4, :].bitcast(I32))
 
         def load_words(dst, src):
             nc.sync.dma_start(dst[:].bitcast(I32), src[0].rearrange("p n t -> p (n t)").bitcast(I32))
 
-        query_view = query.rearrange("(p j) q -> p j q", j=PACK)
+        def by_partition(matrix):
+            return matrix.rearrange("(p j) n -> p j n", j=PACK)
+
+        def four_a_partition(vector):
+            return vector.rearrange("(p r) o -> p (r o)", r=PACK)
+
         for h in range(2):
-            nc.sync.dma_start(query_raw[:, 2 * h:2 * h + 2, :], query_view[:, 2 * h:2 * h + 2, :])
+            nc.sync.dma_start(query_raw[:, 2 * h:2 * h + 2, :], by_partition(query)[:, 2 * h:2 * h + 2, :])
         nc.sync.dma_start(offs_sb[:], offs)
         load_words(key_words, keys_words)
         load_scales(key_scales, keys_scales, 0)
-        nc.sync.dma_start(gout_raw[:], gout.rearrange("(p j) q -> p j q", j=PACK))
+        nc.sync.dma_start(gout_raw[:], by_partition(gout))
         load_scales(val_scales, vals_scales, VAL_ROW)
+        nc.scalar.dma_start(lse_sb[:], four_a_partition(lse))
+        nc.sync.dma_start(qs_sb[:], four_a_partition(qs))
         load_words(val_words, vals_words)
-        nc.sync.dma_start(qrows_raw[:], qrows.rearrange("(p j) d -> p j d", j=PACK))
+        nc.sync.dma_start(delta_sb[:], four_a_partition(delta))
+        nc.sync.dma_start(qrows_raw[:], by_partition(qrows))
         nc.sync.dma_start(offs2_sb[:], offs2)
-        old_view = old.rearrange("(p j) u -> p j u", j=PACK)
-        nc.sync.dma_start(old_first[:], old_view[:, 0, :])
+        nc.sync.dma_start(old_first[:], by_partition(old)[:, 0, :])
         for h in range(2):
-            nc.sync.dma_start(old_rest[h][:], old_view[:, 1:PACK, h * HALF:(h + 1) * HALF])
-        nc.scalar.dma_start(lse_sb[:], lse.rearrange("(p r) o -> p (r o)", r=PACK))
-        nc.scalar.dma_start(qs_sb[:], qs.rearrange("(p r) o -> p (r o)", r=PACK))
-        nc.scalar.dma_start(delta_sb[:], delta.rearrange("(p r) o -> p (r o)", r=PACK))
+            nc.sync.dma_start(old_rest[h][:], by_partition(old)[:, 1:PACK, half(h)])
         nc.gpsimd.memset(fade_rows[:], 0.0)
-        nc.scalar.dma_start(fade_rows[0:U // P, :], fade.rearrange("o (c p) -> (o c) p", p=P))
+        nc.gpsimd.dma_start(fade_rows[0:CHUNKS, :], fade.rearrange("o (c p) -> (o c) p", p=P))
         make_identity(nc, ident[:])
 
         for j in range(PACK):
@@ -102,7 +118,7 @@ def tile_attend_gkeystore_pl_kernel(tc, query, keys_words, keys_scales, gout, va
             codes = tile(name + "_codes", [P, Q], U32)
             scales = tile(name + "_scales", [P, Q], U8)
             quantize(codes[:], scales[:], grouped[:].rearrange("p r m j -> p (r m j)"))
-            return [(codes[:, r * P:(r + 1) * P], scales[:, r * P:(r + 1) * P]) for r in range(PACK)]
+            return [(codes[:, block(r)], scales[:, block(r)]) for r in range(PACK)]
 
         def gather(name, window, dtype):
             picked = tile(name, [P, SLOTS], dtype)
@@ -121,11 +137,11 @@ def tile_attend_gkeystore_pl_kernel(tc, query, keys_words, keys_scales, gout, va
         weights = tile("weights", [P, PACK, SLOTS], F32)
         scaled = tile("scaled", [P, PACK, SLOTS], F32)
         score_banks = [bank(b, "scores%d" % b) for b in range(2)]
+        scores = [score_banks[r // 2][:, (r % 2) * SLOTS:(r % 2 + 1) * SLOTS] for r in range(PACK)]
         for r in range(PACK):
-            product(score_banks[r // 2][:, (r % 2) * SLOTS:(r % 2 + 1) * SLOTS], query_mx[r], keys_mx)
+            product(scores[r], query_mx[r], keys_mx)
         for r in range(PACK):
-            nc.scalar.activation(weights[:, r, :], score_banks[r // 2][:, (r % 2) * SLOTS:(r % 2 + 1) * SLOTS], ACT.Exp,
-                                 bias=neg_lse[:, r:r + 1])
+            nc.scalar.activation(weights[:, r, :], scores[r], ACT.Exp, bias=neg_lse[:, r:r + 1])
         for r in range(PACK):
             nc.scalar.activation(scaled[:, r, :], weights[:, r, :], ACT.Copy, scale=qs_sb[:, r:r + 1])
 
@@ -143,11 +159,12 @@ def tile_attend_gkeystore_pl_kernel(tc, query, keys_words, keys_scales, gout, va
         ds_grouped = tile("ds_grouped", [P, SLOTS * PACK], BF16)
         ds_codes = tile("ds_codes", [P, SLOTS], U32)
         ds_scales = tile("ds_scales", [P, SLOTS], U8)
+        ds_halves = [ds_grouped[:, g * P * PACK:(g + 1) * P * PACK] for g in range(2)]
         for g in range(2):
-            nc.vector.tensor_copy(ds_grouped[:, g * P * PACK:(g + 1) * P * PACK].rearrange("p (c i r) -> p c r i", i=2, r=PACK),
-                                  ds_rows[:, :, g * P:(g + 1) * P].rearrange("p r (c i) -> p c r i", i=2))
+            nc.vector.tensor_copy(ds_halves[g].rearrange("p (c i r) -> p c r i", i=2, r=PACK),
+                                  ds_rows[:, :, block(g)].rearrange("p r (c i) -> p c r i", i=2))
         for g in range(2):
-            quantize(ds_codes[:, g * P:(g + 1) * P], ds_scales[:, g * P:(g + 1) * P], ds_grouped[:, g * P * PACK:(g + 1) * P * PACK])
+            quantize(ds_codes[:, block(g)], ds_scales[:, block(g)], ds_halves[g])
 
         qrows_grouped = tile("qrows_grouped", [P, PACK, P, PACK], BF16)
         for a in range(2):
@@ -156,23 +173,23 @@ def tile_attend_gkeystore_pl_kernel(tc, query, keys_words, keys_scales, gout, va
         first_codes = tile("first_codes", [P, P], U32)
         rest_codes = tile("rest_codes", [P, D - P], U32, tag="ds_grouped")
         qrows_scales = tile("qrows_scales", [P, D], U8)
-        quantize(first_codes[:], qrows_scales[:, P:2 * P], qrows_grouped[:, 1, :, :].rearrange("p m j -> p (m j)"))
-        quantize(rest_codes[:, 0:P], qrows_scales[:, 0:P], qrows_grouped[:, 0, :, :].rearrange("p m j -> p (m j)"))
-        quantize(rest_codes[:, P:3 * P], qrows_scales[:, 2 * P:4 * P], qrows_grouped[:, 2:4, :, :].rearrange("p t m j -> p (t m j)"))
-        qrows_codes = (rest_codes[:, 0:P], first_codes[:], rest_codes[:, P:2 * P], rest_codes[:, 2 * P:3 * P])
-        qrows_mx = [(qrows_codes[j], qrows_scales[:, j * P:(j + 1) * P]) for j in range(PACK)]
+        quantize(first_codes[:], qrows_scales[:, block(1)], qrows_grouped[:, 1, :, :].rearrange("p m j -> p (m j)"))
+        quantize(rest_codes[:, block(0)], qrows_scales[:, block(0)], qrows_grouped[:, 0, :, :].rearrange("p m j -> p (m j)"))
+        quantize(rest_codes[:, P:3 * P], qrows_scales[:, 2 * P:D], qrows_grouped[:, 2:PACK, :, :].rearrange("p t m j -> p (t m j)"))
+        qrows_codes = (rest_codes[:, block(0)], first_codes[:], rest_codes[:, block(1)], rest_codes[:, block(2)])
+        qrows_mx = [(qrows_codes[j], qrows_scales[:, block(j)]) for j in range(PACK)]
 
         fade_bank = bank(6, "fade_bank")
         nc.tensor.transpose(fade_bank[:, 0:P], fade_rows[:], ident[:])
-        fade_cols = tile("fade_cols", [P, U // P], F32)
-        nc.scalar.copy(fade_cols[:], fade_bank[:, 0:U // P])
+        fade_cols = tile("fade_cols", [P, CHUNKS], F32)
+        nc.scalar.copy(fade_cols[:], fade_bank[:, 0:CHUNKS])
         fade_wide = tile("fade_wide", [P, U], F32)
         for h in range(2):
             spread = bank(7 - h, "spread%d" % h)
-            for cc in range(4):
-                c = 4 * h + cc
-                nc.tensor.transpose(spread[:, cc * P:(cc + 1) * P], fade_cols[:, c:c + 1].to_broadcast([P, P]), ident[:])
-            nc.scalar.copy(fade_wide[:, h * HALF:(h + 1) * HALF], spread[:])
+            for cc in range(CHUNKS_A_BANK):
+                c = CHUNKS_A_BANK * h + cc
+                nc.tensor.transpose(spread[:, block(cc)], fade_cols[:, c:c + 1].to_broadcast([P, P]), ident[:])
+            nc.scalar.copy(fade_wide[:, half(h)], spread[:])
 
         pieces = [(1, 0, P, 4), (0, 0, SLOTS, 0), (1, P, SLOTS, 1), (2, 0, SLOTS, 2), (3, 0, SLOTS, 3)]
         dk_banks = [bank(b, "dk%d_%d" % (j, n0)) for j, n0, n1, b in pieces]
@@ -182,69 +199,68 @@ def tile_attend_gkeystore_pl_kernel(tc, query, keys_words, keys_scales, gout, va
         for k, (j, n0, n1, b) in enumerate(pieces):
             nc.scalar.copy(dk_sb[k][:], dk_banks[k][:, 0:n1 - n0])
         for k, (j, n0, n1, b) in enumerate(pieces):
-            nc.vector.tensor_copy(df[j][:].indirect(offs2_sb[:, n0 // 16:n1 // 16]), dk_sb[k][:])
+            nc.vector.tensor_copy(df[j][:].indirect(offs2_sb[:, n0 // LIST_ROWS:n1 // LIST_ROWS]), dk_sb[k][:])
 
         faded_first = tile("faded_first", [P, U], F32, tag="qrows_grouped")
         for h in range(2):
-            nc.gpsimd.tensor_tensor(faded_first[:, h * HALF:(h + 1) * HALF], fade_wide[:, h * HALF:(h + 1) * HALF], old_first[:, h * HALF:(h + 1) * HALF], ALU.mult)
+            nc.gpsimd.tensor_tensor(faded_first[:, half(h)], fade_wide[:, half(h)], old_first[:, half(h)], ALU.mult)
 
-        faded_t = [tile("faded_t%d" % c, [P, PACK - 1, P], F32) for c in range(U // P)]
-        for c in range(U // P):
-            turned = bank(c % 4, "turned%d" % c)
-            for j in range(PACK - 1):
-                nc.tensor.transpose(turned[:, j * P:(j + 1) * P], old_rest[c // 4][:, j, (c % 4) * P:(c % 4 + 1) * P], ident[:])
+        faded_t = [tile("faded_t%d" % c, [P, PACK - 1, P], F32) for c in range(CHUNKS)]
+        for c in range(CHUNKS):
+            turned = bank(c % PACK, "turned%d" % c)
+            for j in range(1, PACK):
+                nc.tensor.transpose(turned[:, block(j - 1)], old_rest[c // CHUNKS_A_BANK][:, j - 1, block(c % CHUNKS_A_BANK)], ident[:])
             nc.scalar.activation(faded_t[c][:].rearrange("p j m -> p (j m)"), turned[:, 0:(PACK - 1) * P], ACT.Copy,
                                  scale=fade_cols[:, c:c + 1])
 
         y = [tile("y%d" % h, [P, PACK, HALF], F32) for h in range(2)]
-        out_view = out_0.rearrange("(p j) u -> p j u", j=PACK)
+        out_planes = by_partition(out_0)
         faded_banks = {}
         faded_second = [tile("faded_second%d" % h, [P, HALF], F32) for h in range(2)]
         for h in range(2):
             for j in range(1, PACK):
-                faded_banks[h, j] = bank(((4, 5, 6), (7, 0, 1))[h][j - 1], "faded%d_%d" % (h, j))
-                for cc in range(4):
-                    nc.tensor.transpose(faded_banks[h, j][:, cc * P:(cc + 1) * P], faded_t[4 * h + cc][:, j - 1, :], ident[:])
+                faded_banks[h, j] = bank((PACK + (PACK - 1) * h + j - 1) % 8, "faded%d_%d" % (h, j))
+                for cc in range(CHUNKS_A_BANK):
+                    nc.tensor.transpose(faded_banks[h, j][:, block(cc)], faded_t[CHUNKS_A_BANK * h + cc][:, j - 1, :], ident[:])
             nc.scalar.copy(faded_second[h][:], faded_banks[h, 1][:])
+
+        faded_sb = [(faded_first[:, half(h)], faded_second[h][:]) for h in range(2)]
         for h in range(2):
-            cols = slice(h * HALF, (h + 1) * HALF)
-            nc.gpsimd.tensor_tensor(y[h][:, 0, :], faded_first[:, cols], df[0][:, cols], ALU.add)
-            nc.sync.dma_start(out_view[:, 0, cols], y[h][:, 0, :])
-        for h in range(2):
-            nc.gpsimd.tensor_tensor(y[h][:, 1, :], faded_second[h][:], df[1][:, h * HALF:(h + 1) * HALF], ALU.add)
-        nc.sync.dma_start(out_view[:, 1, 0:HALF], y[0][:, 1, :])
-        for h, pieces in ((0, ((0, QUARTER), (QUARTER, HALF))), (1, ((0, HALF),))):
-            for n0, n1 in pieces:
-                for j in range(2, PACK):
+            for j in range(GPSIMD_PLANES):
+                nc.gpsimd.tensor_tensor(y[h][:, j, :], faded_sb[h][j], df[j][:, half(h)], ALU.add)
+                if (h, j) != (1, GPSIMD_PLANES - 1):
+                    nc.sync.dma_start(out_planes[:, j, half(h)], y[h][:, j, :])
+        for h, spans in ((0, ((0, QUARTER), (QUARTER, HALF))), (1, ((0, HALF),))):
+            for n0, n1 in spans:
+                for j in range(GPSIMD_PLANES, PACK):
                     nc.vector.tensor_tensor(y[h][:, j, n0:n1], faded_banks[h, j][:, n0:n1], df[j][:, h * HALF + n0:h * HALF + n1], ALU.add)
-            nc.sync.dma_start(out_view[:, 2 - h:PACK, h * HALF:(h + 1) * HALF], y[h][:, 2 - h:PACK, :])
+            nc.sync.dma_start(out_planes[:, GPSIMD_PLANES - h:PACK, half(h)], y[h][:, GPSIMD_PLANES - h:PACK, :])
 
         y_scales = tile("y_scales", [P, U], U8)
-        words_view = out_1[0].rearrange("p n t -> p (n t)").bitcast(I32)
+        out_words = out_1[0].rearrange("p n t -> p (n t)").bitcast(I32)
         y_words = tile("y_words", [P, U], U32)
-        y_grouped = [tile("y_grouped%d" % c, [P, QUARTER, PACK], BF16, tag="faded_t7" if c == 0 else None) for c in range(4)]
+        y_grouped = [tile("y_grouped%d" % v, [P, QUARTER, PACK], BF16, tag="faded_t%d" % (CHUNKS - 1) if v == 0 else None)
+                     for v in range(4)]
 
-        def regroup(c, copy):
-            copy(y_grouped[c][:].rearrange("p (n i) j -> p n j i", i=2),
-                 y[c // 2][:, :, (c % 2) * QUARTER:(c % 2 + 1) * QUARTER].rearrange("p j (n i) -> p n j i", i=2))
+        def regroup(v, copy):
+            copy(y_grouped[v][:].rearrange("p (n i) j -> p n j i", i=2),
+                 y[v // 2][:, :, (v % 2) * QUARTER:(v % 2 + 1) * QUARTER].rearrange("p j (n i) -> p n j i", i=2))
 
-        def quantize_y(c):
-            quantize(y_words[:, c * QUARTER:(c + 1) * QUARTER], y_scales[:, c * QUARTER:(c + 1) * QUARTER],
-                     y_grouped[c][:].rearrange("p n j -> p (n j)"))
+        def quantize_y(v):
+            quantize(y_words[:, v * QUARTER:(v + 1) * QUARTER], y_scales[:, v * QUARTER:(v + 1) * QUARTER],
+                     y_grouped[v][:].rearrange("p n j -> p (n j)"))
 
-        def store_words(c0, c1):
-            nc.sync.dma_start(words_view[:, c0 * QUARTER:c1 * QUARTER], y_words[:, c0 * QUARTER:c1 * QUARTER].bitcast(I32))
+        def store_words(v0, v1):
+            nc.sync.dma_start(out_words[:, v0 * QUARTER:v1 * QUARTER], y_words[:, v0 * QUARTER:v1 * QUARTER].bitcast(I32))
 
-        for c in range(3):
-            regroup(c, nc.scalar.copy)
-        regroup(3, nc.vector.tensor_copy)
-        quantize_y(0)
-        quantize_y(1)
-        store_words(0, 2)
+        for v in (0, 1, 3):
+            regroup(v, nc.scalar.copy)
+        regroup(2, nc.vector.tensor_copy)
+        for v in range(3):
+            quantize_y(v)
+        store_words(0, 3)
         quantize_y(3)
         store_words(3, 4)
-        quantize_y(2)
-        store_words(2, 3)
         for r in range(4):
             queue = nc.sync if r == 0 else nc.scalar
-            queue.dma_start(out_2[0][r:16:4, :].bitcast(I32), y_scales[r:P:32, :].bitcast(I32))
+            queue.dma_start(out_2[0][r:SCALE_ROWS:4, :].bitcast(I32), y_scales[r:P:QUADRANT, :].bitcast(I32))

from contextlib import ExitStack

import concourse.mybir as mybir
from concourse.masks import make_identity

F32 = mybir.dt.float32
BF16 = mybir.dt.bfloat16
I32 = mybir.dt.int32
U32 = mybir.dt.uint32
U16 = mybir.dt.uint16
U8 = mybir.dt.uint8
FP8X4 = mybir.dt.float8_e4m3fn_x4
ALU = mybir.AluOpType
ACT = mybir.ActivationFunctionType

P = 128
PACK = 4
D, E, T, SLOTS, U, Q = 512, 512, 2048, 256, 1024, 512
BANK = 512
HALF = U // 2
QUARTER = U // 4
CHUNKS = U // P
CHUNKS_A_BANK = BANK // P
LIST_ROWS = 16
QUADRANT = 32
SCALE_ROWS = 16
VAL_ROW = 4
GPSIMD_PLANES = 2

FLOPS = 2 * Q * SLOTS * (D + E + D)


def tile_attend_gkeystore_pl_kernel(tc, query, keys_words, keys_scales, gout, vals_words, vals_scales, lse, delta, qs,
                                     qrows, old, fade, offs, offs2, out_0, out_1, out_2):
    nc = tc.nc
    with ExitStack() as ctx:
        sb = ctx.enter_context(tc.tile_pool(name="sb", bufs=1))
        ps = ctx.enter_context(tc.psum_pool(name="ps", bufs=1))

        def tile(name, shape, dtype, tag=None):
            return sb.tile(shape, dtype, name=name, tag=tag or name, align_bytes=64)

        def bank(b, name):
            return ps.tile([P, BANK], F32, name=name, tag="bank%d" % b)

        def half(h):
            return slice(h * HALF, (h + 1) * HALF)

        def block(n):
            return slice(n * P, (n + 1) * P)

        offs_sb = tile("offs_sb", [P, SLOTS // LIST_ROWS], U16)
        offs2_sb = tile("offs2_sb", [P, SLOTS // LIST_ROWS], U16)
        key_words = tile("key_words", [P, T], U32)
        val_words = tile("val_words", [P, T], U32)
        key_scales = tile("key_scales", [P, T], U8)
        val_scales = tile("val_scales", [P, T], U8)
        query_raw = tile("query_raw", [P, PACK, Q], F32)
        gout_raw = tile("gout_raw", [P, PACK, Q], F32)
        qrows_raw = tile("qrows_raw", [P, PACK, D], F32)
        old_first = tile("old_first", [P, U], F32)
        old_rest = [tile("old_rest%d" % h, [P, PACK - 1, HALF], F32) for h in range(2)]
        lse_sb = tile("lse_sb", [P, PACK], F32)
        delta_sb = tile("delta_sb", [P, PACK], F32)
        qs_sb = tile("qs_sb", [P, PACK], F32)
        fade_rows = tile("fade_rows", [P, P], F32)
        ident = tile("ident", [P, P], F32)
        df = [tile("df%d" % j, [P, U], F32) for j in range(PACK)]

        nc.vector.memset(key_scales[:].bitcast(I32), 0)
        nc.vector.memset(val_scales[:].bitcast(I32), 0)

        def load_scales(dst, src, first):
            for r in range(4):
                nc.sync.dma_start(dst[first + r:P:QUADRANT, :].bitcast(I32), src[0][r:SCALE_ROWS:4, :].bitcast(I32))

        def load_words(dst, src):
            nc.sync.dma_start(dst[:].bitcast(I32), src[0].rearrange("p n t -> p (n t)").bitcast(I32))

        def by_partition(matrix):
            return matrix.rearrange("(p j) n -> p j n", j=PACK)

        def four_a_partition(vector):
            return vector.rearrange("(p r) o -> p (r o)", r=PACK)

        for h in range(2):
            nc.sync.dma_start(query_raw[:, 2 * h:2 * h + 2, :], by_partition(query)[:, 2 * h:2 * h + 2, :])
        nc.sync.dma_start(offs_sb[:], offs)
        load_words(key_words, keys_words)
        load_scales(key_scales, keys_scales, 0)
        nc.sync.dma_start(gout_raw[:], by_partition(gout))
        load_scales(val_scales, vals_scales, VAL_ROW)
        nc.scalar.dma_start(lse_sb[:], four_a_partition(lse))
        nc.sync.dma_start(qs_sb[:], four_a_partition(qs))
        load_words(val_words, vals_words)
        nc.sync.dma_start(delta_sb[:], four_a_partition(delta))
        nc.sync.dma_start(qrows_raw[:], by_partition(qrows))
        nc.sync.dma_start(offs2_sb[:], offs2)
        nc.sync.dma_start(old_first[:], by_partition(old)[:, 0, :])
        for h in range(2):
            nc.sync.dma_start(old_rest[h][:], by_partition(old)[:, 1:PACK, half(h)])
        nc.gpsimd.memset(fade_rows[:], 0.0)
        nc.gpsimd.dma_start(fade_rows[0:CHUNKS, :], fade.rearrange("o (c p) -> (o c) p", p=P))
        make_identity(nc, ident[:])

        for j in range(PACK):
            nc.vector.memset(df[j][:], 0.0)

        def quantize(codes, scales, grouped):
            nc.vector.quantize_mx(out=codes.bitcast(FP8X4), scales=scales, in_=grouped)

        def deal(name, raw, copy):
            grouped = tile(name + "_grouped", [P, PACK, P, PACK], BF16)
            copy(grouped[:].rearrange("p (a b) m j -> p a m j b", b=2), raw[:].rearrange("p j (m a b) -> p a m j b", a=2, b=2))
            return grouped

        def quantize_dealt(name, grouped):
            codes = tile(name + "_codes", [P, Q], U32)
            scales = tile(name + "_scales", [P, Q], U8)
            quantize(codes[:], scales[:], grouped[:].rearrange("p r m j -> p (r m j)"))
            return [(codes[:, block(r)], scales[:, block(r)]) for r in range(PACK)]

        def gather(name, window, dtype):
            picked = tile(name, [P, SLOTS], dtype)
            nc.vector.tensor_copy(picked[:], window[:].indirect(offs_sb[:]))
            return picked

        def product(out, stationary, moving):
            nc.tensor.matmul_mx(out=out, lhsT=stationary[0].bitcast(FP8X4), lhsT_scale=stationary[1],
                                rhs=moving[0].bitcast(FP8X4), rhs_scale=moving[1], start=True, stop=True)

        query_grouped = deal("query", query_raw, nc.scalar.copy)
        keys_mx = (gather("picked_key_words", key_words, U32)[:], gather("picked_key_scales", key_scales, U8)[:])
        query_mx = quantize_dealt("query", query_grouped)
        neg_lse = tile("neg_lse", [P, PACK], F32)
        nc.scalar.mul(neg_lse[:], lse_sb[:], -1.0)
        weights = tile("weights", [P, PACK, SLOTS], F32)
        scaled = tile("scaled", [P, PACK, SLOTS], F32)
        score_banks = [bank(b, "scores%d" % b) for b in range(2)]
        scores = [score_banks[r // 2][:, (r % 2) * SLOTS:(r % 2 + 1) * SLOTS] for r in range(PACK)]
        for r in range(PACK):
            product(scores[r], query_mx[r], keys_mx)
        for r in range(PACK):
            nc.scalar.activation(weights[:, r, :], scores[r], ACT.Exp, bias=neg_lse[:, r:r + 1])
        for r in range(PACK):
            nc.scalar.activation(scaled[:, r, :], weights[:, r, :], ACT.Copy, scale=qs_sb[:, r:r + 1])

        gout_grouped = deal("gout", gout_raw, nc.vector.tensor_copy)
        picked_val_scales = gather("picked_val_scales", val_scales, U8)
        gout_mx = quantize_dealt("gout", gout_grouped)
        vals_mx = (gather("picked_val_words", val_words, U32)[:], picked_val_scales[VAL_ROW:P, :])
        ds_rows = tile("ds_rows", [P, PACK, SLOTS], BF16)
        dp_banks = [bank(2 + r, "dp%d" % r) for r in range(PACK)]
        for r in range(PACK):
            product(dp_banks[r][:, 0:SLOTS], gout_mx[r], vals_mx)
        for r in range(PACK):
            nc.vector.scalar_tensor_tensor(ds_rows[:, r, :], dp_banks[r][:, 0:SLOTS], delta_sb[:, r:r + 1], scaled[:, r, :],
                                           ALU.subtract, ALU.mult)
        ds_grouped = tile("ds_grouped", [P, SLOTS * PACK], BF16)
        ds_codes = tile("ds_codes", [P, SLOTS], U32)
        ds_scales = tile("ds_scales", [P, SLOTS], U8)
        ds_halves = [ds_grouped[:, g * P * PACK:(g + 1) * P * PACK] for g in range(2)]
        for g in range(2):
            nc.vector.tensor_copy(ds_halves[g].rearrange("p (c i r) -> p c r i", i=2, r=PACK),
                                  ds_rows[:, :, block(g)].rearrange("p r (c i) -> p c r i", i=2))
        for g in range(2):
            quantize(ds_codes[:, block(g)], ds_scales[:, block(g)], ds_halves[g])

        qrows_grouped = tile("qrows_grouped", [P, PACK, P, PACK], BF16)
        for a in range(2):
            nc.scalar.copy(qrows_grouped[:, 2 * a:2 * a + 2, :, :].rearrange("p b m j -> p m j b"),
                           qrows_raw[:].rearrange("p j (m t) -> p m j t", t=PACK)[:, :, :, 2 * a:2 * a + 2])
        first_codes = tile("first_codes", [P, P], U32)
        rest_codes = tile("rest_codes", [P, D - P], U32, tag="ds_grouped")
        qrows_scales = tile("qrows_scales", [P, D], U8)
        quantize(first_codes[:], qrows_scales[:, block(1)], qrows_grouped[:, 1, :, :].rearrange("p m j -> p (m j)"))
        quantize(rest_codes[:, block(0)], qrows_scales[:, block(0)], qrows_grouped[:, 0, :, :].rearrange("p m j -> p (m j)"))
        quantize(rest_codes[:, P:3 * P], qrows_scales[:, 2 * P:D], qrows_grouped[:, 2:PACK, :, :].rearrange("p t m j -> p (t m j)"))
        qrows_codes = (rest_codes[:, block(0)], first_codes[:], rest_codes[:, block(1)], rest_codes[:, block(2)])
        qrows_mx = [(qrows_codes[j], qrows_scales[:, block(j)]) for j in range(PACK)]

        fade_bank = bank(6, "fade_bank")
        nc.tensor.transpose(fade_bank[:, 0:P], fade_rows[:], ident[:])
        fade_cols = tile("fade_cols", [P, CHUNKS], F32)
        nc.scalar.copy(fade_cols[:], fade_bank[:, 0:CHUNKS])
        fade_wide = tile("fade_wide", [P, U], F32)
        for h in range(2):
            spread = bank(7 - h, "spread%d" % h)
            for cc in range(CHUNKS_A_BANK):
                c = CHUNKS_A_BANK * h + cc
                nc.tensor.transpose(spread[:, block(cc)], fade_cols[:, c:c + 1].to_broadcast([P, P]), ident[:])
            nc.scalar.copy(fade_wide[:, half(h)], spread[:])

        pieces = [(1, 0, P, 4), (0, 0, SLOTS, 0), (1, P, SLOTS, 1), (2, 0, SLOTS, 2), (3, 0, SLOTS, 3)]
        dk_banks = [bank(b, "dk%d_%d" % (j, n0)) for j, n0, n1, b in pieces]
        dk_sb = [tile("dk_sb%d_%d" % (j, n0), [P, n1 - n0], F32) for j, n0, n1, b in pieces]
        for k, (j, n0, n1, b) in enumerate(pieces):
            product(dk_banks[k][:, 0:n1 - n0], qrows_mx[j], (ds_codes[:, n0:n1], ds_scales[:, n0:n1]))
        for k, (j, n0, n1, b) in enumerate(pieces):
            nc.scalar.copy(dk_sb[k][:], dk_banks[k][:, 0:n1 - n0])
        for k, (j, n0, n1, b) in enumerate(pieces):
            nc.vector.tensor_copy(df[j][:].indirect(offs2_sb[:, n0 // LIST_ROWS:n1 // LIST_ROWS]), dk_sb[k][:])

        faded_first = tile("faded_first", [P, U], F32, tag="qrows_grouped")
        for h in range(2):
            nc.gpsimd.tensor_tensor(faded_first[:, half(h)], fade_wide[:, half(h)], old_first[:, half(h)], ALU.mult)

        faded_t = [tile("faded_t%d" % c, [P, PACK - 1, P], F32) for c in range(CHUNKS)]
        for c in range(CHUNKS):
            turned = bank(c % PACK, "turned%d" % c)
            for j in range(1, PACK):
                nc.tensor.transpose(turned[:, block(j - 1)], old_rest[c // CHUNKS_A_BANK][:, j - 1, block(c % CHUNKS_A_BANK)], ident[:])
            nc.scalar.activation(faded_t[c][:].rearrange("p j m -> p (j m)"), turned[:, 0:(PACK - 1) * P], ACT.Copy,
                                 scale=fade_cols[:, c:c + 1])

        y = [tile("y%d" % h, [P, PACK, HALF], F32) for h in range(2)]
        out_planes = by_partition(out_0)
        faded_banks = {}
        faded_second = [tile("faded_second%d" % h, [P, HALF], F32) for h in range(2)]
        for h in range(2):
            for j in range(1, PACK):
                faded_banks[h, j] = bank((PACK + (PACK - 1) * h + j - 1) % 8, "faded%d_%d" % (h, j))
                for cc in range(CHUNKS_A_BANK):
                    nc.tensor.transpose(faded_banks[h, j][:, block(cc)], faded_t[CHUNKS_A_BANK * h + cc][:, j - 1, :], ident[:])
            nc.scalar.copy(faded_second[h][:], faded_banks[h, 1][:])

        faded_sb = [(faded_first[:, half(h)], faded_second[h][:]) for h in range(2)]
        for h in range(2):
            for j in range(GPSIMD_PLANES):
                nc.gpsimd.tensor_tensor(y[h][:, j, :], faded_sb[h][j], df[j][:, half(h)], ALU.add)
                if (h, j) != (1, GPSIMD_PLANES - 1):
                    nc.sync.dma_start(out_planes[:, j, half(h)], y[h][:, j, :])
        for h, spans in ((0, ((0, QUARTER), (QUARTER, HALF))), (1, ((0, HALF),))):
            for n0, n1 in spans:
                for j in range(GPSIMD_PLANES, PACK):
                    nc.vector.tensor_tensor(y[h][:, j, n0:n1], faded_banks[h, j][:, n0:n1], df[j][:, h * HALF + n0:h * HALF + n1], ALU.add)
            nc.sync.dma_start(out_planes[:, GPSIMD_PLANES - h:PACK, half(h)], y[h][:, GPSIMD_PLANES - h:PACK, :])

        y_scales = tile("y_scales", [P, U], U8)
        out_words = out_1[0].rearrange("p n t -> p (n t)").bitcast(I32)
        y_words = tile("y_words", [P, U], U32)
        y_grouped = [tile("y_grouped%d" % v, [P, QUARTER, PACK], BF16, tag="faded_t%d" % (CHUNKS - 1) if v == 0 else None)
                     for v in range(4)]

        def regroup(v, copy):
            copy(y_grouped[v][:].rearrange("p (n i) j -> p n j i", i=2),
                 y[v // 2][:, :, (v % 2) * QUARTER:(v % 2 + 1) * QUARTER].rearrange("p j (n i) -> p n j i", i=2))

        def quantize_y(v):
            quantize(y_words[:, v * QUARTER:(v + 1) * QUARTER], y_scales[:, v * QUARTER:(v + 1) * QUARTER],
                     y_grouped[v][:].rearrange("p n j -> p (n j)"))

        def store_words(v0, v1):
            nc.sync.dma_start(out_words[:, v0 * QUARTER:v1 * QUARTER], y_words[:, v0 * QUARTER:v1 * QUARTER].bitcast(I32))

        for v in (0, 1, 3):
            regroup(v, nc.scalar.copy)
        regroup(2, nc.vector.tensor_copy)
        for v in range(3):
            quantize_y(v)
        store_words(0, 3)
        quantize_y(3)
        store_words(3, 4)
        for r in range(4):
            queue = nc.sync if r == 0 else nc.scalar
            queue.dma_start(out_2[0][r:SCALE_ROWS:4, :].bitcast(I32), y_scales[r:P:QUADRANT, :].bitcast(I32))
